import numpy as np
import ml_dtypes


def mxq(x, axis, fmt="e4m3"):
    dtype, down = {"e4m3": (ml_dtypes.float8_e4m3fn, 7), "e5m2": (ml_dtypes.float8_e5m2, 14)}[fmt]
    v = np.moveaxis(np.asarray(x, np.float32).astype(ml_dtypes.bfloat16).astype(np.float64), axis, -1)
    blocks = v.reshape(v.shape[:-1] + (-1, 32))
    amax = np.abs(blocks).max(-1, keepdims=True)
    byte = np.maximum(np.where(amax > 0, np.frexp(amax)[1] - 1 + 127, 0) - down, 1)
    scale = np.exp2(byte - 127.0)
    codes = (blocks / scale).astype(np.float32).astype(dtype).astype(np.float64)
    return np.moveaxis((codes * scale).reshape(v.shape), -1, axis)


WIDE = False


def mx_kscale(k):
    if not WIDE:
        return np.ones(k)
    levels = np.array([10, -10, 5, -5, 0])
    if k % 512:
        return np.exp2(np.random.permutation(np.resize(levels, k // 32))).repeat(32)
    a = np.empty((k // 512, 16))
    for p in range(k // 512):
        a[p, :8] = np.random.permutation(np.resize(levels, 8))
        for g in range(8):
            far = levels[np.abs(levels - a[p, g]) >= 10]
            a[p, g + 8] = far[np.random.randint(len(far))]
    return np.exp2(a.ravel()).repeat(32)


def f64(x):
    return np.asarray(x).astype(np.float64)


def striped8(idx):
    return np.asarray(idx).reshape(8, -1, 16).transpose(0, 2, 1).reshape(128, -1).astype(np.uint16)


def unstriped8(offs):
    return offs.reshape(8, 16, -1).transpose(0, 2, 1).reshape(8, -1).astype(np.int64)


def pick8(x, idx, run):
    r = np.arange(len(x))
    return x[r[:, None], idx[r % (8 * run) // run]]


E2M1 = np.array([0.0, 0.5, 1.0, 1.5, 2.0, 3.0, 4.0, 6.0, -0.0, -0.5, -1.0, -1.5, -2.0, -3.0, -4.0, -6.0])


def pack_weight(w, fmt):
    k, n = w.shape
    w = f64(np.asarray(w, np.float32).astype(ml_dtypes.bfloat16)).reshape(k // 32, 32, n)
    amax = np.abs(w).max(1)
    if fmt == "e4m3":
        byte = np.frexp(amax)[1] - 1 + 127 - 7
    else:
        mant, ex = np.frexp(amax / 6.0)
        byte = np.where(mant > 0.5, ex, ex - 1) + 127
    byte = np.clip(np.where(amax > 0, byte, 1), 1, 254)
    scaled = (w * np.exp2(127.0 - byte)[:, None, :]).reshape(k, n).astype(np.float32)
    by_word = np.ascontiguousarray(scaled.reshape(k // 512, 128, 4, n).transpose(0, 1, 3, 2))
    if fmt == "e4m3":
        words = by_word.astype(ml_dtypes.float8_e4m3fn).view(np.uint8)
    else:
        c = by_word.astype(ml_dtypes.float4_e2m1fn).view(np.uint8) & 0xF
        words = (c[..., 0::2] | (c[..., 1::2] << 4)).reshape(k // 512, 128, 2 * n)
    return np.ascontiguousarray(words), np.ascontiguousarray(byte.astype(np.uint8).reshape(k // 512, 16, n))


def unpack_weight(words, scales, fmt):
    g, _, n = scales.shape
    words = np.ascontiguousarray(words).reshape(g, 128, n, -1)
    if fmt == "e4m3":
        vals = words.view(ml_dtypes.float8_e4m3fn).astype(np.float64)
    else:
        nib = np.empty((g, 128, n, 4), np.uint8)
        nib[..., 0::2] = words & 0xF
        nib[..., 1::2] = words >> 4
        vals = E2M1[nib]
    vals = vals * np.repeat(np.exp2(scales.astype(np.float64) - 127.0), 8, axis=1)[..., None]
    return vals.transpose(0, 1, 3, 2).reshape(g * 512, n)


D, T, U, X, S, I, Q = 512, 1024, 1024, 1024, 1024, 512, 128


def setup_inputs():
    n = np.random.standard_normal
    idx = np.stack([np.random.permutation(T)[:I] for _ in range(8)])
    idx2 = np.stack([np.random.permutation(U)[:I] for _ in range(8)])
    idx3 = np.stack([np.random.permutation(X)[:I] for _ in range(8)])
    idx4 = np.stack([np.random.permutation(S)[:I] for _ in range(8)])
    idx5 = np.stack([np.random.permutation(U)[:I] for _ in range(8)])
    idx6 = np.stack([np.random.permutation(S)[:I] for _ in range(8)])
    idx7 = np.stack([np.random.permutation(T)[:I] for _ in range(8)])
    fd = mx_kscale(D)
    cachep = pack_weight(n((D, T)) / fd[:, None], "e4m3")
    draftp = pack_weight(n((D, U)) / fd[:, None], "e2m1")
    archp = pack_weight(n((D, X)) / fd[:, None], "e4m3")
    prefp = pack_weight(n((D, S)) / fd[:, None], "e2m1")
    return {
        "query": (n((D, Q)) * 1.0 / np.sqrt(D) * fd[:, None]).astype(np.float32),
        "query2": (n((D, Q)) * 1.0 / np.sqrt(D) * fd[:, None]).astype(np.float32),
        "cache_words": cachep[0],
        "cache_scales": cachep[1],
        "draft_words": draftp[0],
        "draft_scales": draftp[1],
        "arch_words": archp[0],
        "arch_scales": archp[1],
        "pref_words": prefp[0],
        "pref_scales": prefp[1],
        "offs": striped8(idx),
        "offs2": striped8(idx2),
        "offs3": striped8(idx3),
        "offs4": striped8(idx4),
        "offs5": striped8(idx5),
        "offs6": striped8(idx6),
        "offs7": striped8(idx7),
    }


def reference(query, query2, cache_words, cache_scales, draft_words, draft_scales, arch_words, arch_scales, pref_words, pref_scales, offs, offs2, offs3, offs4, offs5, offs6, offs7):
    idx = unstriped8(offs)
    idx2 = unstriped8(offs2)
    idx3 = unstriped8(offs3)
    idx4 = unstriped8(offs4)
    idx5 = unstriped8(offs5)
    idx6 = unstriped8(offs6)
    idx7 = unstriped8(offs7)
    cacheu = unpack_weight(cache_words, cache_scales, "e4m3")
    draftu = unpack_weight(draft_words, draft_scales, "e2m1")
    archu = unpack_weight(arch_words, arch_scales, "e4m3")
    prefu = unpack_weight(pref_words, pref_scales, "e2m1")
    queryq = mxq(f64(query), 0, "e4m3")
    a = queryq.T @ cacheu
    b = queryq.T @ draftu
    query2q = mxq(f64(query2), 0, "e4m3")
    c0 = query2q.T @ archu
    d0 = query2q.T @ prefu
    f1 = np.zeros((Q, U))
    f1[np.arange(Q)[:, None], idx2[np.arange(Q) % 128 // 16]] = pick8(a, idx, 16)
    f2 = np.zeros((Q, S))
    f2[np.arange(Q)[:, None], idx4[np.arange(Q) % 128 // 16]] = pick8(c0, idx3, 16)
    bb = b + f1
    dd = d0 - f2
    v = np.maximum(pick8(bb, idx5, 16), pick8(dd, idx6, 16))
    f3 = np.zeros((Q, T))
    f3[np.arange(Q)[:, None], idx7[np.arange(Q) % 128 // 16]] = v
    aa = a + f3
    y = pick8(aa, idx, 16)
    return y

@@ -1,0 +1,169 @@
+from contextlib import ExitStack
+
+import concourse.mybir as mybir
+
+F32 = mybir.dt.float32
+BF16 = mybir.dt.bfloat16
+I32 = mybir.dt.int32
+U32 = mybir.dt.uint32
+U16 = mybir.dt.uint16
+U8 = mybir.dt.uint8
+FP8X4 = mybir.dt.float8_e4m3fn_x4
+FP4X4 = mybir.dt.float4_e2m1fn_x4
+COPY = mybir.ActivationFunctionType.Copy
+ALU = mybir.AluOpType
+
+P = 128
+PACK = 4
+ROWS = 128
+TOKENS = 1024
+SLOTS = 512
+BANK = 512
+HALF = SLOTS // 2
+LIST_COLS = SLOTS // 16
+FLOPS = 4 * 2 * 512 * ROWS * TOKENS
+
+
+def tile_attend_fourring_fourtwo_kernel(tc, query, query2, cache_words, cache_scales, draft_words, draft_scales,
+                                         arch_words, arch_scales, pref_words, pref_scales,
+                                         offs, offs2, offs3, offs4, offs5, offs6, offs7, out):
+    nc = tc.nc
+    with ExitStack() as ctx:
+        lists = ctx.enter_context(tc.tile_pool(name="lists", bufs=1))
+        sb = ctx.enter_context(tc.tile_pool(name="sb", bufs=1))
+        psum = ctx.enter_context(tc.psum_pool(name="psum", bufs=1))
+
+        def load_list(name, src):
+            t = lists.tile([P, LIST_COLS], U16, name=name)
+            nc.sync.dma_start(t[:], src)
+            return t
+
+        def load_query(name, src):
+            raw = sb.tile([P, PACK, ROWS], F32, name=name + "_raw", align_bytes=64)
+            nc.sync.dma_start(raw[:], src.rearrange("(p j) q -> p j q", j=PACK))
+            return raw
+
+        def quantise(name, raw):
+            grouped = sb.tile([P, ROWS, PACK], BF16, name=name + "_bf16", align_bytes=64)
+            codes = sb.tile([P, ROWS], U32, name=name + "_codes", align_bytes=64)
+            plane = sb.tile([P, ROWS], U8, name=name + "_plane", align_bytes=64)
+            nc.vector.tensor_copy(grouped[:], raw[:].rearrange("p j q -> p q j"))
+            nc.vector.quantize_mx(out=codes[:].bitcast(FP8X4), scales=plane[:],
+                                  in_=grouped[:].rearrange("p q j -> p (q j)"))
+            return codes, plane
+
+        def zeroed_plane(name):
+            plane = sb.tile([P, TOKENS], U8, name=name + "_plane", align_bytes=64)
+            return plane
+
+        def load_scales(plane, src):
+            rows = src[0].bitcast(I32)
+            for quad in range(4):
+                nc.sync.dma_start(plane[32 * quad:32 * quad + 4, :].bitcast(I32), rows[4 * quad:4 * quad + 4, :])
+
+        def load_fp8(name, src):
+            words = sb.tile([P, TOKENS], U32, name=name + "_words", align_bytes=256)
+            nc.sync.dma_start(words[:].bitcast(I32), src[0].rearrange("p n t -> p (n t)").bitcast(I32))
+            return lambda c0, c1: words[:, c0:c1].bitcast(FP8X4)
+
+        def load_fp4(name, src):
+            words = sb.tile([P, 2 * TOKENS], U8, name=name + "_words", align_bytes=256)
+            nc.sync.dma_start(words[:].bitcast(I32), src[0].bitcast(I32))
+            return lambda c0, c1: words[:, 2 * c0:2 * c1].bitcast(FP4X4)
+
+        def scores(tags, q, keys, plane, widths):
+            codes, qplane = q
+            banks = []
+            c0 = 0
+            for tag, width in zip(tags, widths):
+                bank = psum.tile([P, width], F32, name=tag)
+                nc.tensor.matmul_mx(out=bank[:], lhsT=codes[:].bitcast(FP8X4), lhsT_scale=qplane[:],
+                                    rhs=keys(c0, c0 + width), rhs_scale=plane[:, c0:c0 + width], start=True, stop=True)
+                banks.append((bank, slice(c0, c0 + width)))
+                c0 = c0 + width
+            return banks
+
+        def zeroed_window(name, engine, tag):
+            window = sb.tile([P, TOKENS], F32, name=name, tag=tag)
+            engine.memset(window[:], 0.0)
+            return window
+
+        def part(h):
+            return slice(h * HALF, (h + 1) * HALF), slice(h * LIST_COLS // 2, (h + 1) * LIST_COLS // 2)
+
+        def combine(name, banks, window, op):
+            total = sb.tile([P, TOKENS], F32, name=name, tag="table")
+            for bank, cols in banks:
+                nc.vector.tensor_tensor(total[:, cols], bank[:], window[:, cols], op)
+            return total
+
+        cache_plane = zeroed_plane("cache")
+        arch_plane = zeroed_plane("arch")
+        draft_plane = zeroed_plane("draft")
+        pref_plane = zeroed_plane("pref")
+        f1 = zeroed_window("f1", nc.vector, "f1")
+        f2 = zeroed_window("f2", nc.vector, "f2")
+        f3a = zeroed_window("f3a", nc.gpsimd, "f3a")
+
+        q1_raw = load_query("q1", query)
+        load_scales(cache_plane, cache_scales)
+        cache = load_fp8("cache", cache_words)
+        q2_raw = load_query("q2", query2)
+        l1 = load_list("l1", offs)
+        l2 = load_list("l2", offs2)
+        load_scales(arch_plane, arch_scales)
+        arch = load_fp8("arch", arch_words)
+        l3 = load_list("l3", offs3)
+        l4 = load_list("l4", offs4)
+        load_scales(draft_plane, draft_scales)
+        draft = load_fp4("draft", draft_words)
+        l5 = load_list("l5", offs5)
+        load_scales(pref_plane, pref_scales)
+        pref = load_fp4("pref", pref_words)
+        l6 = load_list("l6", offs6)
+        l7 = load_list("l7", offs7)
+
+        q1 = quantise("q1", q1_raw)
+        a_banks = scores(("p0", "p1", "p2"), q1, cache, cache_plane, (512, 256, 256))
+        q2 = quantise("q2", q2_raw)
+        a = sb.tile([P, TOKENS], F32, name="a")
+        nc.vector.tensor_copy(a[:, a_banks[0][1]], a_banks[0][0][:])
+        nc.scalar.copy(a[:, a_banks[1][1]], a_banks[1][0][:])
+        nc.scalar.copy(a[:, a_banks[2][1]], a_banks[2][0][:])
+        a_picked = sb.tile([P, SLOTS], F32, name="a_picked", tag="a_picked")
+        nc.vector.tensor_copy(a_picked[:, part(0)[0]], a[:].indirect(l1[:, part(0)[1]]))
+        nc.scalar.activation(a_picked[:, part(1)[0]], a[:].indirect(l1[:, part(1)[1]]), COPY)
+        nc.scalar.activation(f1[:].indirect(l2[:]), a_picked[:], COPY)
+        c_banks = scores(("p3", "p4"), q2, arch, arch_plane, (512, 512))
+        c0 = sb.tile([P, TOKENS], F32, name="c0", tag="table")
+        for bank, cols in c_banks:
+            nc.vector.tensor_copy(c0[:, cols], bank[:])
+        c_picked = sb.tile([P, SLOTS], F32, name="c_picked")
+        nc.vector.tensor_copy(c_picked[:], c0[:].indirect(l3[:]))
+        nc.scalar.activation(f2[:].indirect(l4[:]), c_picked[:], COPY)
+        f3b = zeroed_window("f3b", nc.gpsimd, "a_picked")
+
+        b_banks = scores(("p5", "p6"), q1, draft, draft_plane, (512, 512))
+        d_banks = scores(("p7", "p0"), q2, pref, pref_plane, (512, 512))
+        bb = combine("bb", b_banks, f1, ALU.add)
+        bb_picked = sb.tile([P, SLOTS], F32, name="bb_picked")
+        nc.vector.tensor_copy(bb_picked[:], bb[:].indirect(l5[:]))
+        dd = combine("dd", d_banks, f2, ALU.subtract)
+        for h, f3 in enumerate((f3a, f3b)):
+            slots, cols = part(h)
+            dd_picked = sb.tile([P, HALF], F32, name="dd_picked%d" % h, tag="dd_picked")
+            v = sb.tile([P, HALF], F32, name="v%d" % h)
+            nc.vector.tensor_copy(dd_picked[:], dd[:].indirect(l6[:, cols]))
+            nc.vector.tensor_tensor(v[:], bb_picked[:, slots], dd_picked[:], ALU.max)
+            nc.scalar.activation(f3[:].indirect(l7[:, cols]), v[:], COPY)
+
+        partial = sb.tile([P, TOKENS], F32, name="partial")
+        aa = sb.tile([P, TOKENS], F32, name="aa")
+        nc.vector.tensor_tensor(partial[:], a[:], f3a[:], ALU.add)
+        nc.vector.tensor_tensor(aa[:], partial[:], f3b[:], ALU.add)
+        y0 = sb.tile([P, HALF], F32, name="y0")
+        y1 = sb.tile([P, HALF], F32, name="y1")
+        nc.vector.tensor_copy(y0[:], aa[:].indirect(l1[:, part(0)[1]]))
+        nc.scalar.activation(y1[:], aa[:].indirect(l1[:, part(1)[1]]), COPY)
+        nc.sync.dma_start(out[:, part(0)[0]], y0[:])
+        nc.scalar.dma_start(out[:, part(1)[0]], y1[:])

@@ -20,6 +20,7 @@ TOKENS = 1024
 SLOTS = 512
 BANK = 512
 HALF = SLOTS // 2
+FIRST = 128
 LIST_COLS = SLOTS // 16
 FLOPS = 4 * 2 * 512 * ROWS * TOKENS
 
@@ -43,11 +44,16 @@ def tile_attend_fourring_fourtwo_kernel(tc, query, query2, cache_words, cache_sc
             nc.sync.dma_start(raw[:], src.rearrange("(p j) q -> p j q", j=PACK))
             return raw
 
-        def quantise(name, raw):
+        def rounded(name, raw):
             grouped = sb.tile([P, ROWS, PACK], BF16, name=name + "_bf16", align_bytes=64)
+            src = raw[:].rearrange("p j q -> p q j")
+            nc.vector.tensor_copy(grouped[:, :ROWS // 2, :], src[:, :ROWS // 2, :])
+            nc.scalar.copy(grouped[:, ROWS // 2:, :], src[:, ROWS // 2:, :])
+            return grouped
+
+        def quantise(name, grouped):
             codes = sb.tile([P, ROWS], U32, name=name + "_codes", align_bytes=64)
             plane = sb.tile([P, ROWS], U8, name=name + "_plane", align_bytes=64)
-            nc.vector.tensor_copy(grouped[:], raw[:].rearrange("p j q -> p q j"))
             nc.vector.quantize_mx(out=codes[:].bitcast(FP8X4), scales=plane[:],
                                   in_=grouped[:].rearrange("p q j -> p (q j)"))
             return codes, plane
@@ -61,9 +67,12 @@ def tile_attend_fourring_fourtwo_kernel(tc, query, query2, cache_words, cache_sc
             for quad in range(4):
                 nc.sync.dma_start(plane[32 * quad:32 * quad + 4, :].bitcast(I32), rows[4 * quad:4 * quad + 4, :])
 
-        def load_fp8(name, src):
+        def load_fp8(name, src, pieces):
             words = sb.tile([P, TOKENS], U32, name=name + "_words", align_bytes=256)
-            nc.sync.dma_start(words[:].bitcast(I32), src[0].rearrange("p n t -> p (n t)").bitcast(I32))
+            rows = src[0].rearrange("p n t -> p (n t)").bitcast(I32)
+            width = TOKENS // pieces
+            for c0 in range(0, TOKENS, width):
+                nc.sync.dma_start(words[:, c0:c0 + width].bitcast(I32), rows[:, c0:c0 + width])
             return lambda c0, c1: words[:, c0:c1].bitcast(FP8X4)
 
         def load_fp4(name, src):
@@ -103,16 +112,15 @@ def tile_attend_fourring_fourtwo_kernel(tc, query, query2, cache_words, cache_sc
         pref_plane = zeroed_plane("pref")
         f1 = zeroed_window("f1", nc.vector, "f1")
         f2 = zeroed_window("f2", nc.vector, "f2")
-        f3a = zeroed_window("f3a", nc.gpsimd, "f3a")
 
         q1_raw = load_query("q1", query)
         load_scales(cache_plane, cache_scales)
-        cache = load_fp8("cache", cache_words)
+        cache = load_fp8("cache", cache_words, 2)
         q2_raw = load_query("q2", query2)
         l1 = load_list("l1", offs)
-        l2 = load_list("l2", offs2)
         load_scales(arch_plane, arch_scales)
-        arch = load_fp8("arch", arch_words)
+        arch = load_fp8("arch", arch_words, 2)
+        l2 = load_list("l2", offs2)
         l3 = load_list("l3", offs3)
         l4 = load_list("l4", offs4)
         load_scales(draft_plane, draft_scales)
@@ -123,39 +131,42 @@ def tile_attend_fourring_fourtwo_kernel(tc, query, query2, cache_words, cache_sc
         l6 = load_list("l6", offs6)
         l7 = load_list("l7", offs7)
 
-        q1 = quantise("q1", q1_raw)
-        a_banks = scores(("p0", "p1", "p2"), q1, cache, cache_plane, (512, 256, 256))
-        q2 = quantise("q2", q2_raw)
+        q1 = quantise("q1", rounded("q1", q1_raw))
+        a_banks = scores(("p0", "p1", "p2", "p3"), q1, cache, cache_plane, (512, 256, 128, 128))
+        q2_grouped = rounded("q2", q2_raw)
         a = sb.tile([P, TOKENS], F32, name="a")
         nc.vector.tensor_copy(a[:, a_banks[0][1]], a_banks[0][0][:])
+        q2 = quantise("q2", q2_grouped)
         nc.scalar.copy(a[:, a_banks[1][1]], a_banks[1][0][:])
         nc.scalar.copy(a[:, a_banks[2][1]], a_banks[2][0][:])
+        nc.vector.tensor_copy(a[:, a_banks[3][1]], a_banks[3][0][:])
         a_picked = sb.tile([P, SLOTS], F32, name="a_picked", tag="a_picked")
         nc.vector.tensor_copy(a_picked[:, part(0)[0]], a[:].indirect(l1[:, part(0)[1]]))
         nc.scalar.activation(a_picked[:, part(1)[0]], a[:].indirect(l1[:, part(1)[1]]), COPY)
         nc.scalar.activation(f1[:].indirect(l2[:]), a_picked[:], COPY)
-        c_banks = scores(("p3", "p4"), q2, arch, arch_plane, (512, 512))
-        c0 = sb.tile([P, TOKENS], F32, name="c0", tag="table")
+        c_banks = scores(("p4", "p5"), q2, arch, arch_plane, (512, 512))
+        c0 = sb.tile([P, TOKENS], F32, name="c0", tag="c0")
         for bank, cols in c_banks:
             nc.vector.tensor_copy(c0[:, cols], bank[:])
         c_picked = sb.tile([P, SLOTS], F32, name="c_picked")
         nc.vector.tensor_copy(c_picked[:], c0[:].indirect(l3[:]))
         nc.scalar.activation(f2[:].indirect(l4[:]), c_picked[:], COPY)
+        f3a = zeroed_window("f3a", nc.gpsimd, "c0")
         f3b = zeroed_window("f3b", nc.gpsimd, "a_picked")
 
-        b_banks = scores(("p5", "p6"), q1, draft, draft_plane, (512, 512))
-        d_banks = scores(("p7", "p0"), q2, pref, pref_plane, (512, 512))
+        b_banks = scores(("p4", "p5"), q1, draft, draft_plane, (512, 512))
+        d_banks = scores(("p6", "p7"), q2, pref, pref_plane, (512, 512))
         bb = combine("bb", b_banks, f1, ALU.add)
         bb_picked = sb.tile([P, SLOTS], F32, name="bb_picked")
         nc.vector.tensor_copy(bb_picked[:], bb[:].indirect(l5[:]))
         dd = combine("dd", d_banks, f2, ALU.subtract)
-        for h, f3 in enumerate((f3a, f3b)):
-            slots, cols = part(h)
-            dd_picked = sb.tile([P, HALF], F32, name="dd_picked%d" % h, tag="dd_picked")
-            v = sb.tile([P, HALF], F32, name="v%d" % h)
-            nc.vector.tensor_copy(dd_picked[:], dd[:].indirect(l6[:, cols]))
-            nc.vector.tensor_tensor(v[:], bb_picked[:, slots], dd_picked[:], ALU.max)
-            nc.scalar.activation(f3[:].indirect(l7[:, cols]), v[:], COPY)
+        dd_picked = sb.tile([P, SLOTS], F32, name="dd_picked")
+        nc.vector.tensor_copy(dd_picked[:, part(0)[0]], dd[:].indirect(l6[:, part(0)[1]]))
+        nc.scalar.activation(dd_picked[:, part(1)[0]], dd[:].indirect(l6[:, part(1)[1]]), COPY)
+        v = sb.tile([P, SLOTS], F32, name="v")
+        for f3, s0, s1 in ((f3a, 0, FIRST), (f3b, FIRST, SLOTS)):
+            nc.vector.tensor_tensor(v[:, s0:s1], bb_picked[:, s0:s1], dd_picked[:, s0:s1], ALU.max)
+            nc.scalar.activation(f3[:].indirect(l7[:, s0 // 16:s1 // 16]), v[:, s0:s1], COPY)
 
         partial = sb.tile([P, TOKENS], F32, name="partial")
         aa = sb.tile([P, TOKENS], F32, name="aa")

from contextlib import ExitStack

import concourse.mybir as mybir

F32 = mybir.dt.float32
BF16 = mybir.dt.bfloat16
I32 = mybir.dt.int32
U32 = mybir.dt.uint32
U16 = mybir.dt.uint16
U8 = mybir.dt.uint8
FP8X4 = mybir.dt.float8_e4m3fn_x4
FP4X4 = mybir.dt.float4_e2m1fn_x4
COPY = mybir.ActivationFunctionType.Copy
ALU = mybir.AluOpType

P = 128
PACK = 4
ROWS = 128
TOKENS = 1024
SLOTS = 512
BANK = 512
HALF = SLOTS // 2
FIRST = 128
LIST_COLS = SLOTS // 16
FLOPS = 4 * 2 * 512 * ROWS * TOKENS


def tile_attend_fourring_fourtwo_kernel(tc, query, query2, cache_words, cache_scales, draft_words, draft_scales,
                                         arch_words, arch_scales, pref_words, pref_scales,
                                         offs, offs2, offs3, offs4, offs5, offs6, offs7, out):
    nc = tc.nc
    with ExitStack() as ctx:
        lists = ctx.enter_context(tc.tile_pool(name="lists", bufs=1))
        sb = ctx.enter_context(tc.tile_pool(name="sb", bufs=1))
        psum = ctx.enter_context(tc.psum_pool(name="psum", bufs=1))

        def load_list(name, src):
            t = lists.tile([P, LIST_COLS], U16, name=name)
            nc.sync.dma_start(t[:], src)
            return t

        def load_query(name, src):
            raw = sb.tile([P, PACK, ROWS], F32, name=name + "_raw", align_bytes=64)
            nc.sync.dma_start(raw[:], src.rearrange("(p j) q -> p j q", j=PACK))
            return raw

        def rounded(name, raw):
            grouped = sb.tile([P, ROWS, PACK], BF16, name=name + "_bf16", align_bytes=64)
            src = raw[:].rearrange("p j q -> p q j")
            nc.vector.tensor_copy(grouped[:, :ROWS // 2, :], src[:, :ROWS // 2, :])
            nc.scalar.copy(grouped[:, ROWS // 2:, :], src[:, ROWS // 2:, :])
            return grouped

        def quantise(name, grouped):
            codes = sb.tile([P, ROWS], U32, name=name + "_codes", align_bytes=64)
            plane = sb.tile([P, ROWS], U8, name=name + "_plane", align_bytes=64)
            nc.vector.quantize_mx(out=codes[:].bitcast(FP8X4), scales=plane[:],
                                  in_=grouped[:].rearrange("p q j -> p (q j)"))
            return codes, plane

        def zeroed_plane(name):
            plane = sb.tile([P, TOKENS], U8, name=name + "_plane", align_bytes=64)
            return plane

        def load_scales(plane, src):
            rows = src[0].bitcast(I32)
            for quad in range(4):
                nc.sync.dma_start(plane[32 * quad:32 * quad + 4, :].bitcast(I32), rows[4 * quad:4 * quad + 4, :])

        def load_fp8(name, src, pieces):
            words = sb.tile([P, TOKENS], U32, name=name + "_words", align_bytes=256)
            rows = src[0].rearrange("p n t -> p (n t)").bitcast(I32)
            width = TOKENS // pieces
            for c0 in range(0, TOKENS, width):
                nc.sync.dma_start(words[:, c0:c0 + width].bitcast(I32), rows[:, c0:c0 + width])
            return lambda c0, c1: words[:, c0:c1].bitcast(FP8X4)

        def load_fp4(name, src):
            words = sb.tile([P, 2 * TOKENS], U8, name=name + "_words", align_bytes=256)
            nc.sync.dma_start(words[:].bitcast(I32), src[0].bitcast(I32))
            return lambda c0, c1: words[:, 2 * c0:2 * c1].bitcast(FP4X4)

        def scores(tags, q, keys, plane, widths):
            codes, qplane = q
            banks = []
            c0 = 0
            for tag, width in zip(tags, widths):
                bank = psum.tile([P, width], F32, name=tag)
                nc.tensor.matmul_mx(out=bank[:], lhsT=codes[:].bitcast(FP8X4), lhsT_scale=qplane[:],
                                    rhs=keys(c0, c0 + width), rhs_scale=plane[:, c0:c0 + width], start=True, stop=True)
                banks.append((bank, slice(c0, c0 + width)))
                c0 = c0 + width
            return banks

        def zeroed_window(name, engine, tag):
            window = sb.tile([P, TOKENS], F32, name=name, tag=tag)
            engine.memset(window[:], 0.0)
            return window

        def part(h):
            return slice(h * HALF, (h + 1) * HALF), slice(h * LIST_COLS // 2, (h + 1) * LIST_COLS // 2)

        def combine(name, banks, window, op):
            total = sb.tile([P, TOKENS], F32, name=name, tag="table")
            for bank, cols in banks:
                nc.vector.tensor_tensor(total[:, cols], bank[:], window[:, cols], op)
            return total

        cache_plane = zeroed_plane("cache")
        arch_plane = zeroed_plane("arch")
        draft_plane = zeroed_plane("draft")
        pref_plane = zeroed_plane("pref")
        f1 = zeroed_window("f1", nc.vector, "f1")
        f2 = zeroed_window("f2", nc.vector, "f2")

        q1_raw = load_query("q1", query)
        load_scales(cache_plane, cache_scales)
        cache = load_fp8("cache", cache_words, 2)
        q2_raw = load_query("q2", query2)
        l1 = load_list("l1", offs)
        load_scales(arch_plane, arch_scales)
        arch = load_fp8("arch", arch_words, 2)
        l2 = load_list("l2", offs2)
        l3 = load_list("l3", offs3)
        l4 = load_list("l4", offs4)
        load_scales(draft_plane, draft_scales)
        draft = load_fp4("draft", draft_words)
        l5 = load_list("l5", offs5)
        load_scales(pref_plane, pref_scales)
        pref = load_fp4("pref", pref_words)
        l6 = load_list("l6", offs6)
        l7 = load_list("l7", offs7)

        q1 = quantise("q1", rounded("q1", q1_raw))
        a_banks = scores(("p0", "p1", "p2", "p3"), q1, cache, cache_plane, (512, 256, 128, 128))
        q2_grouped = rounded("q2", q2_raw)
        a = sb.tile([P, TOKENS], F32, name="a")
        nc.vector.tensor_copy(a[:, a_banks[0][1]], a_banks[0][0][:])
        q2 = quantise("q2", q2_grouped)
        nc.scalar.copy(a[:, a_banks[1][1]], a_banks[1][0][:])
        nc.scalar.copy(a[:, a_banks[2][1]], a_banks[2][0][:])
        nc.vector.tensor_copy(a[:, a_banks[3][1]], a_banks[3][0][:])
        a_picked = sb.tile([P, SLOTS], F32, name="a_picked", tag="a_picked")
        nc.vector.tensor_copy(a_picked[:, part(0)[0]], a[:].indirect(l1[:, part(0)[1]]))
        nc.scalar.activation(a_picked[:, part(1)[0]], a[:].indirect(l1[:, part(1)[1]]), COPY)
        nc.scalar.activation(f1[:].indirect(l2[:]), a_picked[:], COPY)
        c_banks = scores(("p4", "p5"), q2, arch, arch_plane, (512, 512))
        c0 = sb.tile([P, TOKENS], F32, name="c0", tag="c0")
        for bank, cols in c_banks:
            nc.vector.tensor_copy(c0[:, cols], bank[:])
        c_picked = sb.tile([P, SLOTS], F32, name="c_picked")
        nc.vector.tensor_copy(c_picked[:], c0[:].indirect(l3[:]))
        nc.scalar.activation(f2[:].indirect(l4[:]), c_picked[:], COPY)
        f3a = zeroed_window("f3a", nc.gpsimd, "c0")
        f3b = zeroed_window("f3b", nc.gpsimd, "a_picked")

        b_banks = scores(("p4", "p5"), q1, draft, draft_plane, (512, 512))
        d_banks = scores(("p6", "p7"), q2, pref, pref_plane, (512, 512))
        bb = combine("bb", b_banks, f1, ALU.add)
        bb_picked = sb.tile([P, SLOTS], F32, name="bb_picked")
        nc.vector.tensor_copy(bb_picked[:], bb[:].indirect(l5[:]))
        dd = combine("dd", d_banks, f2, ALU.subtract)
        dd_picked = sb.tile([P, SLOTS], F32, name="dd_picked")
        nc.vector.tensor_copy(dd_picked[:, part(0)[0]], dd[:].indirect(l6[:, part(0)[1]]))
        nc.scalar.activation(dd_picked[:, part(1)[0]], dd[:].indirect(l6[:, part(1)[1]]), COPY)
        v = sb.tile([P, SLOTS], F32, name="v")
        for f3, s0, s1 in ((f3a, 0, FIRST), (f3b, FIRST, SLOTS)):
            nc.vector.tensor_tensor(v[:, s0:s1], bb_picked[:, s0:s1], dd_picked[:, s0:s1], ALU.max)
            nc.scalar.activation(f3[:].indirect(l7[:, s0 // 16:s1 // 16]), v[:, s0:s1], COPY)

        partial = sb.tile([P, TOKENS], F32, name="partial")
        aa = sb.tile([P, TOKENS], F32, name="aa")
        nc.vector.tensor_tensor(partial[:], a[:], f3a[:], ALU.add)
        nc.vector.tensor_tensor(aa[:], partial[:], f3b[:], ALU.add)
        y0 = sb.tile([P, HALF], F32, name="y0")
        y1 = sb.tile([P, HALF], F32, name="y1")
        nc.vector.tensor_copy(y0[:], aa[:].indirect(l1[:, part(0)[1]]))
        nc.scalar.activation(y1[:], aa[:].indirect(l1[:, part(1)[1]]), COPY)
        nc.sync.dma_start(out[:, part(0)[0]], y0[:])
        nc.scalar.dma_start(out[:, part(1)[0]], y1[:])
